import numpy as np
import ml_dtypes


def mxq(x, axis, fmt="e4m3"):
    dtype, down = {"e4m3": (ml_dtypes.float8_e4m3fn, 7), "e5m2": (ml_dtypes.float8_e5m2, 14)}[fmt]
    v = np.moveaxis(np.asarray(x, np.float32).astype(ml_dtypes.bfloat16).astype(np.float64), axis, -1)
    blocks = v.reshape(v.shape[:-1] + (-1, 32))
    amax = np.abs(blocks).max(-1, keepdims=True)
    byte = np.maximum(np.where(amax > 0, np.frexp(amax)[1] - 1 + 127, 0) - down, 1)
    scale = np.exp2(byte - 127.0)
    codes = (blocks / scale).astype(np.float32).astype(dtype).astype(np.float64)
    return np.moveaxis((codes * scale).reshape(v.shape), -1, axis)


WIDE = False


def mx_kscale(k):
    if not WIDE:
        return np.ones(k)
    levels = np.array([30, -30])
    if k % 512:
        return np.exp2(np.random.permutation(np.resize(levels, k // 32))).repeat(32)
    a = np.empty((k // 512, 16))
    for p in range(k // 512):
        a[p, :8] = np.random.permutation(np.resize(levels, 8))
        for g in range(8):
            far = levels[np.abs(levels - a[p, g]) >= 10]
            a[p, g + 8] = far[np.random.randint(len(far))]
    return np.exp2(a.ravel()).repeat(32)


def f64(x):
    return np.asarray(x).astype(np.float64)


def striped(idx):
    return np.tile(np.asarray(idx).reshape(-1, 16).T, (8, 1)).astype(np.uint16)


def unstriped(offs):
    return offs[:16].T.reshape(-1).astype(np.int64)


E2M1 = np.array([0.0, 0.5, 1.0, 1.5, 2.0, 3.0, 4.0, 6.0, -0.0, -0.5, -1.0, -1.5, -2.0, -3.0, -4.0, -6.0])


def pack_weight(w, fmt):
    k, n = w.shape
    w = f64(np.asarray(w, np.float32).astype(ml_dtypes.bfloat16)).reshape(k // 32, 32, n)
    amax = np.abs(w).max(1)
    if fmt in ("e4m3", "e5m2"):
        byte = np.frexp(amax)[1] - 1 + 127 - (7 if fmt == "e4m3" else 14)
    else:
        mant, ex = np.frexp(amax / 6.0)
        byte = np.where(mant > 0.5, ex, ex - 1) + 127
    byte = np.clip(np.where(amax > 0, byte, 1), 1, 254)
    scaled = (w * np.exp2(127.0 - byte)[:, None, :]).reshape(k, n).astype(np.float32)
    by_word = np.ascontiguousarray(scaled.reshape(k // 512, 128, 4, n).transpose(0, 1, 3, 2))
    if fmt in ("e4m3", "e5m2"):
        words = by_word.astype(ml_dtypes.float8_e4m3fn if fmt == "e4m3" else ml_dtypes.float8_e5m2).view(np.uint8)
    else:
        c = by_word.astype(ml_dtypes.float4_e2m1fn).view(np.uint8) & 0xF
        words = (c[..., 0::2] | (c[..., 1::2] << 4)).reshape(k // 512, 128, 2 * n)
    return np.ascontiguousarray(words), np.ascontiguousarray(byte.astype(np.uint8).reshape(k // 512, 16, n))


def unpack_weight(words, scales, fmt):
    g, _, n = scales.shape
    words = np.ascontiguousarray(words).reshape(g, 128, n, -1)
    if fmt in ("e4m3", "e5m2"):
        vals = words.view(ml_dtypes.float8_e4m3fn if fmt == "e4m3" else ml_dtypes.float8_e5m2).astype(np.float64)
    else:
        nib = np.empty((g, 128, n, 4), np.uint8)
        nib[..., 0::2] = words & 0xF
        nib[..., 1::2] = words >> 4
        vals = E2M1[nib]
    vals = vals * np.repeat(np.exp2(scales.astype(np.float64) - 127.0), 8, axis=1)[..., None]
    return vals.transpose(0, 1, 3, 2).reshape(g * 512, n)


K, T, J, R, C, N = 512, 2048, 256, 512, 512, 256


def setup_inputs():
    n = np.random.standard_normal
    idx = np.random.permutation(T)[:J]
    idx2 = np.random.permutation(T)[:J]
    idx3 = np.random.permutation(C)[:J]
    idx4 = np.random.permutation(C)[:J]
    fk = mx_kscale(K)
    fr = mx_kscale(R)
    xtp = pack_weight(n((K, T)) / fk[:, None], "e5m2")
    wp = pack_weight(n((K, R)) * 1 / np.sqrt(K) * fk[:, None] * fr, "e2m1")
    w2p = pack_weight(n((K, R)) * 1 / np.sqrt(K) * fk[:, None] * fr, "e4m3")
    wbp = pack_weight(n((R, N)) * 1 / np.sqrt(R) / fr[:, None], "e2m1")
    wsp = pack_weight(n((K, N)) * 1 / np.sqrt(K) * fk[:, None], "e2m1")
    return {
        "xt_words": xtp[0],
        "xt_scales": xtp[1],
        "w_words": wp[0],
        "w_scales": wp[1],
        "w2_words": w2p[0],
        "w2_scales": w2p[1],
        "wb_words": wbp[0],
        "wb_scales": wbp[1],
        "ws_words": wsp[0],
        "ws_scales": wsp[1],
        "offs": striped(idx),
        "offs2": striped(idx2),
        "offs3": striped(idx3),
        "offs4": striped(idx4),
    }


def reference(xt_words, xt_scales, w_words, w_scales, w2_words, w2_scales, wb_words, wb_scales, ws_words, ws_scales, offs, offs2, offs3, offs4):
    idx = unstriped(offs)
    idx2 = unstriped(offs2)
    idx3 = unstriped(offs3)
    idx4 = unstriped(offs4)
    xtu = unpack_weight(xt_words, xt_scales, "e5m2")
    wu = unpack_weight(w_words, w_scales, "e2m1")
    w2u = unpack_weight(w2_words, w2_scales, "e4m3")
    wbu = unpack_weight(wb_words, wb_scales, "e2m1")
    wsu = unpack_weight(ws_words, ws_scales, "e2m1")
    xtidxg = xtu[:, idx]
    a = wu.T @ xtidxg
    xtidx2g = xtu[:, idx2]
    b = w2u.T @ xtidx2g
    pw = np.zeros((R, C))
    pw[:, idx3] = a
    hid = np.maximum(pw[:, idx4], b)
    hidq = mxq(hid, 0, "e4m3")
    y = wbu.T @ hidq + wsu.T @ xtidxg
    return y

@@ -1,0 +1,190 @@
+from contextlib import ExitStack
+
+import concourse.mybir as mybir
+
+K, T, J, R, C, N = 512, 2048, 256, 512, 512, 256
+FLOPS = 2 * J * (2 * K * R + R * N + K * N)
+
+F32 = mybir.dt.float32
+BF16 = mybir.dt.bfloat16
+I32 = mybir.dt.int32
+U32 = mybir.dt.uint32
+U16 = mybir.dt.uint16
+U8 = mybir.dt.uint8
+E4M3 = mybir.dt.float8_e4m3fn_x4
+E5M2 = mybir.dt.float8_e5m2_x4
+E2M1 = mybir.dt.float4_e2m1fn_x4
+COPY = mybir.ActivationFunctionType.Copy
+MAX = mybir.AluOpType.max
+
+P = 128
+PACK = 4
+HALF = J // 2
+LIST_COLS = J // 16
+
+
+def tile_list_ahead_board_skip_plain_kernel(
+    tc, xt_words, xt_scales, w_words, w_scales, w2_words, w2_scales, wb_words, wb_scales,
+    ws_words, ws_scales, offs, offs2, offs3, offs4, out,
+):
+    nc = tc.nc
+    with ExitStack() as ctx:
+        sb = ctx.enter_context(tc.tile_pool(name="sb", bufs=1))
+        ps = ctx.enter_context(tc.psum_pool(name="ps", bufs=1))
+
+        def tile(name, cols, dtype, tag=None):
+            return sb.tile([P] + cols, dtype, name=name, tag=tag or name, align_bytes=64)
+
+        def load_scale_rows(queues, plane, scales):
+            for q, queue in enumerate(queues):
+                queue.dma_start(plane[32 * q : 32 * q + 4, :].bitcast(I32), scales[0, 4 * q : 4 * q + 4, :].bitcast(I32))
+
+        first = sb.tile([P, LIST_COLS], U16, name="first")
+        second = sb.tile([P, LIST_COLS], U16, name="second")
+        put = sb.tile([P, LIST_COLS], U16, name="put")
+        read = sb.tile([P, LIST_COLS], U16, name="read")
+        x_words = tile("x_words", [T], U32)
+        x_plane = tile("x_plane", [T], U8)
+        w_raw = tile("w_raw", [2 * R], U8, "raw")
+        wb_sb = tile("wb_sb", [2 * N], U8)
+        ws_sb = tile("ws_sb", [2 * N], U8)
+        w_plane = tile("w_plane", [R], U8, "early")
+        planes = tile("planes", [R + 2 * N], U8)
+        w2_plane = planes[:, 0:R]
+        ws_plane = planes[:, R : R + N]
+        wb_plane = planes[:, R + N : R + 2 * N]
+        boards = [tile("board%d" % t, [C], F32) for t in range(PACK)]
+
+        nc.vector.memset(x_plane[:].bitcast(I32), 0)
+        nc.vector.memset(w_plane[:].bitcast(I32), 0)
+        nc.vector.memset(planes[:].bitcast(I32), 0)
+        for board in boards:
+            nc.vector.memset(board[:], 0.0)
+
+        nc.scalar.dma_start(w_raw[:].bitcast(I32), w_words[0].bitcast(I32))
+        nc.sync.dma_start(first[:], offs)
+        nc.sync.dma_start(second[:], offs2)
+        load_scale_rows([nc.sync, nc.sync, nc.scalar, nc.scalar], x_plane, xt_scales)
+        nc.sync.dma_start(x_words[:].bitcast(I32), xt_words[0].rearrange("p c r -> p (c r)").bitcast(I32))
+        on_sync = [nc.sync] * 4
+        load_scale_rows(on_sync, w_plane, w_scales)
+        nc.sync.dma_start(put[:], offs3)
+        nc.sync.dma_start(read[:], offs4)
+        load_scale_rows([nc.gpsimd] * 4, w2_plane, w2_scales)
+        nc.sync.dma_start(ws_sb[:].bitcast(I32), ws_words[0].bitcast(I32))
+        nc.sync.dma_start(wb_sb[:].bitcast(I32), wb_words[0].bitcast(I32))
+        load_scale_rows(on_sync, ws_plane, ws_scales)
+        load_scale_rows(on_sync, wb_plane, wb_scales)
+
+        w_dealt = tile("w_dealt", [2 * R], U8)
+        w2_dealt = tile("w2_dealt", [R], U32)
+        plane_dealt = tile("plane_dealt", [R], U8)
+
+        def deal(copy, dealt, raw):
+            copy(dealt.rearrange("p (t m) -> p t m", t=PACK), raw.rearrange("p (m t) -> p t m", t=PACK))
+
+        x1 = tile("x1", [J], U32)
+        s1 = tile("s1", [J], U8)
+        s2 = tile("s2", [J], U8)
+
+        deal(nc.scalar.copy, w_dealt[:].bitcast(U16), w_raw[:].bitcast(U16))
+        w2_raw = tile("w2_raw", [R], U32, "raw")
+        nc.scalar.dma_start(w2_raw[:].bitcast(I32), w2_words[0].rearrange("p c r -> p (c r)").bitcast(I32))
+        nc.vector.tensor_copy(s1[:], x_plane[:].indirect(first[:]))
+        nc.vector.tensor_copy(s2[:], x_plane[:].indirect(second[:]))
+        nc.vector.tensor_copy(x1[:], x_words[:].indirect(first[:]))
+        for t0 in (0, 2):
+            nc.vector.tensor_copy(
+                plane_dealt[:].rearrange("p (t m) -> p t m", t=PACK)[:, t0 : t0 + 2, :],
+                w_plane[:].rearrange("p (m t) -> p t m", t=PACK)[:, t0 : t0 + 2, :])
+        x2 = tile("x2", [J], U32, "early")
+        nc.vector.tensor_copy(x2[:], x_words[:].indirect(second[:]))
+        deal(nc.scalar.copy, w2_dealt[:], w2_raw[:])
+
+        a_ps = [ps.tile([P, J], F32, name="a_ps%d" % t, tag="a_ps%d" % t) for t in range(PACK)]
+        a_sb = [tile("a_sb%d" % t, [J], F32) for t in range(PACK)]
+        for t in range(PACK):
+            nc.tensor.matmul_mx(
+                a_ps[t][:], lhsT=w_dealt[:, 2 * P * t : 2 * P * (t + 1)].bitcast(E2M1),
+                lhsT_scale=plane_dealt[:, P * t : P * (t + 1)],
+                rhs=x1[:].bitcast(E5M2), rhs_scale=s1[:], start=True, stop=True)
+
+        def on_scalar(dst, src):
+            nc.scalar.activation(dst, src, COPY)
+
+        on_vector = nc.vector.tensor_copy
+
+        def leave(move, t):
+            move(a_sb[t][:], a_ps[t][:])
+
+        def place(move, t):
+            move(boards[t][:].indirect(put[:]), a_sb[t][:])
+
+        picked = [tile("picked%d" % h, [PACK, HALF], F32) for h in range(2)]
+
+        def pick(move, t, h):
+            cols = LIST_COLS // 2
+            move(picked[h][:, t, :], boards[t][:].indirect(read[:, cols * h : cols * (h + 1)]))
+
+        leave(on_scalar, 0)
+        place(on_scalar, 0)
+        leave(on_vector, 1)
+        place(on_vector, 1)
+        leave(on_scalar, 2)
+        pick(on_scalar, 0, 0)
+        place(on_scalar, 2)
+        leave(on_vector, 3)
+        deal(on_vector, plane_dealt[:], w2_plane)
+        place(on_vector, 3)
+
+        b_ps = [ps.tile([P, PACK, HALF], F32, name="b_ps%d" % h) for h in range(2)]
+        y_tags = [["y_ps0", "y_ps1"], ["a_ps0", "a_ps1"]]
+        y_ps = [[ps.tile([P, HALF], F32, name="y_ps%d%d" % (h, n), tag=y_tags[h][n]) for n in range(2)] for h in range(2)]
+        halves = [slice(HALF * h, HALF * (h + 1)) for h in range(2)]
+        for h in range(2):
+            for t in range(PACK):
+                nc.tensor.matmul_mx(
+                    b_ps[h][:, t, :], lhsT=w2_dealt[:, P * t : P * (t + 1)].bitcast(E4M3),
+                    lhsT_scale=plane_dealt[:, P * t : P * (t + 1)],
+                    rhs=x2[:, halves[h]].bitcast(E5M2), rhs_scale=s2[:, halves[h]], start=True, stop=True)
+        for h in range(2):
+            for n in range(2):
+                nc.tensor.matmul_mx(
+                    y_ps[h][n][:], lhsT=ws_sb[:, 2 * P * n : 2 * P * (n + 1)].bitcast(E2M1),
+                    lhsT_scale=ws_plane[:, P * n : P * (n + 1)],
+                    rhs=x1[:, halves[h]].bitcast(E5M2), rhs_scale=s1[:, halves[h]], start=True, stop=False)
+
+        hid = [tile("hid%d" % h, [PACK * HALF], BF16) for h in range(2)]
+        codes = [tile("codes%d" % h, [HALF], U32) for h in range(2)]
+        h_plane = [tile("h_plane%d" % h, [HALF], U8) for h in range(2)]
+        y_sb = [tile("y_sb%d" % h, [2, HALF], F32) for h in range(2)]
+        out_v = out.rearrange("(n p) j -> p n j", p=P)
+
+        def larger(h):
+            nc.vector.tensor_tensor(
+                hid[h][:].rearrange("p (c i t) -> p c t i", i=4, t=PACK),
+                picked[h][:].rearrange("p t (c i) -> p c t i", i=4),
+                b_ps[h][:].rearrange("p t (c i) -> p c t i", i=4), MAX)
+
+        def finish(h, moves):
+            nc.vector.quantize_mx(codes[h][:].bitcast(E4M3), h_plane[h][:], hid[h][:])
+            for n in range(2):
+                nc.tensor.matmul_mx(
+                    y_ps[h][n][:], lhsT=wb_sb[:, 2 * P * n : 2 * P * (n + 1)].bitcast(E2M1),
+                    lhsT_scale=wb_plane[:, P * n : P * (n + 1)],
+                    rhs=codes[h][:].bitcast(E4M3), rhs_scale=h_plane[h][:], start=False, stop=True)
+            for n in range(2):
+                moves[n](y_sb[h][:, n, :], y_ps[h][n][:])
+            nc.sync.dma_start(out_v[:, :, halves[h]], y_sb[h][:])
+
+        pick(on_scalar, 1, 0)
+        pick(on_scalar, 2, 0)
+        pick(on_vector, 3, 0)
+        larger(0)
+        pick(on_scalar, 0, 1)
+        pick(on_scalar, 1, 1)
+        pick(on_scalar, 2, 1)
+        pick(on_vector, 3, 1)
+        finish(0, [on_scalar, on_scalar])
+        larger(1)
+        finish(1, [on_scalar, on_vector])

@@ -45,17 +45,19 @@ def tile_list_ahead_board_skip_plain_kernel(
         read = sb.tile([P, LIST_COLS], U16, name="read")
         x_words = tile("x_words", [T], U32)
         x_plane = tile("x_plane", [T], U8)
-        w_raw = tile("w_raw", [2 * R], U8, "raw")
+        w_raw = tile("w_raw", [2 * R], U8)
+        w2_raw = tile("w2_raw", [R], U32, "raw")
         wb_sb = tile("wb_sb", [2 * N], U8)
         ws_sb = tile("ws_sb", [2 * N], U8)
         w_plane = tile("w_plane", [R], U8, "early")
-        planes = tile("planes", [R + 2 * N], U8)
-        w2_plane = planes[:, 0:R]
-        ws_plane = planes[:, R : R + N]
-        wb_plane = planes[:, R + N : R + 2 * N]
+        w2_plane = tile("w2_plane", [R], U8, "late")
+        planes = tile("planes", [2 * N], U8)
+        ws_plane = planes[:, 0:N]
+        wb_plane = planes[:, N : 2 * N]
         boards = [tile("board%d" % t, [C], F32) for t in range(PACK)]
 
         nc.vector.memset(x_plane[:].bitcast(I32), 0)
+        nc.vector.memset(w2_plane[:].bitcast(I32), 0)
         nc.vector.memset(w_plane[:].bitcast(I32), 0)
         nc.vector.memset(planes[:].bitcast(I32), 0)
         for board in boards:
@@ -69,8 +71,9 @@ def tile_list_ahead_board_skip_plain_kernel(
         on_sync = [nc.sync] * 4
         load_scale_rows(on_sync, w_plane, w_scales)
         nc.sync.dma_start(put[:], offs3)
+        nc.sync.dma_start(w2_raw[:].bitcast(I32), w2_words[0].rearrange("p c r -> p (c r)").bitcast(I32))
+        load_scale_rows([nc.gpsimd] * 2 + [nc.sync] * 2, w2_plane, w2_scales)
         nc.sync.dma_start(read[:], offs4)
-        load_scale_rows([nc.gpsimd] * 4, w2_plane, w2_scales)
         nc.sync.dma_start(ws_sb[:].bitcast(I32), ws_words[0].bitcast(I32))
         nc.sync.dma_start(wb_sb[:].bitcast(I32), wb_words[0].bitcast(I32))
         load_scale_rows(on_sync, ws_plane, ws_scales)
@@ -83,27 +86,32 @@ def tile_list_ahead_board_skip_plain_kernel(
         def deal(copy, dealt, raw):
             copy(dealt.rearrange("p (t m) -> p t m", t=PACK), raw.rearrange("p (m t) -> p t m", t=PACK))
 
+        def deal_words(dealt, raw):
+            nc.scalar.copy(dealt.rearrange("p (t m) -> p m t", t=PACK), raw.rearrange("p (m t) -> p m t", t=PACK))
+
         x1 = tile("x1", [J], U32)
         s1 = tile("s1", [J], U8)
         s2 = tile("s2", [J], U8)
 
-        deal(nc.scalar.copy, w_dealt[:].bitcast(U16), w_raw[:].bitcast(U16))
-        w2_raw = tile("w2_raw", [R], U32, "raw")
-        nc.scalar.dma_start(w2_raw[:].bitcast(I32), w2_words[0].rearrange("p c r -> p (c r)").bitcast(I32))
+        deal_words(w_dealt[:].bitcast(U16), w_raw[:].bitcast(U16))
         nc.vector.tensor_copy(s1[:], x_plane[:].indirect(first[:]))
         nc.vector.tensor_copy(s2[:], x_plane[:].indirect(second[:]))
         nc.vector.tensor_copy(x1[:], x_words[:].indirect(first[:]))
-        for t0 in (0, 2):
+        for t0 in range(2):
             nc.vector.tensor_copy(
-                plane_dealt[:].rearrange("p (t m) -> p t m", t=PACK)[:, t0 : t0 + 2, :],
-                w_plane[:].rearrange("p (m t) -> p t m", t=PACK)[:, t0 : t0 + 2, :])
+                plane_dealt[:].rearrange("p (t m) -> p t m", t=PACK)[:, t0::2, :],
+                w_plane[:].rearrange("p (m t) -> p t m", t=PACK)[:, t0::2, :])
         x2 = tile("x2", [J], U32, "early")
         nc.vector.tensor_copy(x2[:], x_words[:].indirect(second[:]))
-        deal(nc.scalar.copy, w2_dealt[:], w2_raw[:])
+        deal_words(w2_dealt[:], w2_raw[:])
 
         a_ps = [ps.tile([P, J], F32, name="a_ps%d" % t, tag="a_ps%d" % t) for t in range(PACK)]
-        a_sb = [tile("a_sb%d" % t, [J], F32) for t in range(PACK)]
-        for t in range(PACK):
+        a_even = tile("a_even", [2 * J], F32, "raw")
+        plane2_dealt = tile("plane2_dealt", [R], U8)
+        deal(nc.vector.tensor_copy, plane2_dealt[:], w2_plane[:])
+        a_odd = tile("a_odd", [2 * J], F32, "late")
+        a_sb = [(a_even, a_odd)[t % 2][:, J * (t // 2) : J * (t // 2 + 1)] for t in range(PACK)]
+        for t in (0, 2, 1, 3):
             nc.tensor.matmul_mx(
                 a_ps[t][:], lhsT=w_dealt[:, 2 * P * t : 2 * P * (t + 1)].bitcast(E2M1),
                 lhsT_scale=plane_dealt[:, P * t : P * (t + 1)],
@@ -115,10 +123,10 @@ def tile_list_ahead_board_skip_plain_kernel(
         on_vector = nc.vector.tensor_copy
 
         def leave(move, t):
-            move(a_sb[t][:], a_ps[t][:])
+            move(a_sb[t], a_ps[t][:])
 
         def place(move, t):
-            move(boards[t][:].indirect(put[:]), a_sb[t][:])
+            move(boards[t][:].indirect(put[:]), a_sb[t])
 
         picked = [tile("picked%d" % h, [PACK, HALF], F32) for h in range(2)]
 
@@ -126,16 +134,9 @@ def tile_list_ahead_board_skip_plain_kernel(
             cols = LIST_COLS // 2
             move(picked[h][:, t, :], boards[t][:].indirect(read[:, cols * h : cols * (h + 1)]))
 
-        leave(on_scalar, 0)
-        place(on_scalar, 0)
-        leave(on_vector, 1)
-        place(on_vector, 1)
-        leave(on_scalar, 2)
-        pick(on_scalar, 0, 0)
-        place(on_scalar, 2)
-        leave(on_vector, 3)
-        deal(on_vector, plane_dealt[:], w2_plane)
-        place(on_vector, 3)
+        for step in (leave, place):
+            for t in range(PACK):
+                step((on_scalar, on_vector)[t % 2], t)
 
         b_ps = [ps.tile([P, PACK, HALF], F32, name="b_ps%d" % h) for h in range(2)]
         y_tags = [["y_ps0", "y_ps1"], ["a_ps0", "a_ps1"]]
@@ -145,7 +146,7 @@ def tile_list_ahead_board_skip_plain_kernel(
             for t in range(PACK):
                 nc.tensor.matmul_mx(
                     b_ps[h][:, t, :], lhsT=w2_dealt[:, P * t : P * (t + 1)].bitcast(E4M3),
-                    lhsT_scale=plane_dealt[:, P * t : P * (t + 1)],
+                    lhsT_scale=plane2_dealt[:, P * t : P * (t + 1)],
                     rhs=x2[:, halves[h]].bitcast(E5M2), rhs_scale=s2[:, halves[h]], start=True, stop=True)
         for h in range(2):
             for n in range(2):
@@ -166,25 +167,22 @@ def tile_list_ahead_board_skip_plain_kernel(
                 picked[h][:].rearrange("p t (c i) -> p c t i", i=4),
                 b_ps[h][:].rearrange("p t (c i) -> p c t i", i=4), MAX)
 
-        def finish(h, moves):
+        def finish(h):
             nc.vector.quantize_mx(codes[h][:].bitcast(E4M3), h_plane[h][:], hid[h][:])
             for n in range(2):
                 nc.tensor.matmul_mx(
                     y_ps[h][n][:], lhsT=wb_sb[:, 2 * P * n : 2 * P * (n + 1)].bitcast(E2M1),
                     lhsT_scale=wb_plane[:, P * n : P * (n + 1)],
                     rhs=codes[h][:].bitcast(E4M3), rhs_scale=h_plane[h][:], start=False, stop=True)
-            for n in range(2):
-                moves[n](y_sb[h][:, n, :], y_ps[h][n][:])
+
+        def store(h):
+            on_scalar(y_sb[h][:, 0, :], y_ps[h][0][:])
+            on_vector(y_sb[h][:, 1, :], y_ps[h][1][:])
             nc.sync.dma_start(out_v[:, :, halves[h]], y_sb[h][:])
 
-        pick(on_scalar, 1, 0)
-        pick(on_scalar, 2, 0)
-        pick(on_vector, 3, 0)
-        larger(0)
-        pick(on_scalar, 0, 1)
-        pick(on_scalar, 1, 1)
-        pick(on_scalar, 2, 1)
-        pick(on_vector, 3, 1)
-        finish(0, [on_scalar, on_scalar])
-        larger(1)
-        finish(1, [on_scalar, on_vector])
+        for h in range(2):
+            for t in range(PACK):
+                pick(on_vector if t == 3 or (t, h) == (1, 0) else on_scalar, t, h)
+        for step in (larger, finish, store):
+            for h in range(2):
+                step(h)

from contextlib import ExitStack

import concourse.mybir as mybir

K, T, J, R, C, N = 512, 2048, 256, 512, 512, 256
FLOPS = 2 * J * (2 * K * R + R * N + K * N)

F32 = mybir.dt.float32
BF16 = mybir.dt.bfloat16
I32 = mybir.dt.int32
U32 = mybir.dt.uint32
U16 = mybir.dt.uint16
U8 = mybir.dt.uint8
E4M3 = mybir.dt.float8_e4m3fn_x4
E5M2 = mybir.dt.float8_e5m2_x4
E2M1 = mybir.dt.float4_e2m1fn_x4
COPY = mybir.ActivationFunctionType.Copy
MAX = mybir.AluOpType.max

P = 128
PACK = 4
HALF = J // 2
LIST_COLS = J // 16


def tile_list_ahead_board_skip_plain_kernel(
    tc, xt_words, xt_scales, w_words, w_scales, w2_words, w2_scales, wb_words, wb_scales,
    ws_words, ws_scales, offs, offs2, offs3, offs4, out,
):
    nc = tc.nc
    with ExitStack() as ctx:
        sb = ctx.enter_context(tc.tile_pool(name="sb", bufs=1))
        ps = ctx.enter_context(tc.psum_pool(name="ps", bufs=1))

        def tile(name, cols, dtype, tag=None):
            return sb.tile([P] + cols, dtype, name=name, tag=tag or name, align_bytes=64)

        def load_scale_rows(queues, plane, scales):
            for q, queue in enumerate(queues):
                queue.dma_start(plane[32 * q : 32 * q + 4, :].bitcast(I32), scales[0, 4 * q : 4 * q + 4, :].bitcast(I32))

        first = sb.tile([P, LIST_COLS], U16, name="first")
        second = sb.tile([P, LIST_COLS], U16, name="second")
        put = sb.tile([P, LIST_COLS], U16, name="put")
        read = sb.tile([P, LIST_COLS], U16, name="read")
        x_words = tile("x_words", [T], U32)
        x_plane = tile("x_plane", [T], U8)
        w_raw = tile("w_raw", [2 * R], U8)
        w2_raw = tile("w2_raw", [R], U32, "raw")
        wb_sb = tile("wb_sb", [2 * N], U8)
        ws_sb = tile("ws_sb", [2 * N], U8)
        w_plane = tile("w_plane", [R], U8, "early")
        w2_plane = tile("w2_plane", [R], U8, "late")
        planes = tile("planes", [2 * N], U8)
        ws_plane = planes[:, 0:N]
        wb_plane = planes[:, N : 2 * N]
        boards = [tile("board%d" % t, [C], F32) for t in range(PACK)]

        nc.vector.memset(x_plane[:].bitcast(I32), 0)
        nc.vector.memset(w2_plane[:].bitcast(I32), 0)
        nc.vector.memset(w_plane[:].bitcast(I32), 0)
        nc.vector.memset(planes[:].bitcast(I32), 0)
        for board in boards:
            nc.vector.memset(board[:], 0.0)

        nc.scalar.dma_start(w_raw[:].bitcast(I32), w_words[0].bitcast(I32))
        nc.sync.dma_start(first[:], offs)
        nc.sync.dma_start(second[:], offs2)
        load_scale_rows([nc.sync, nc.sync, nc.scalar, nc.scalar], x_plane, xt_scales)
        nc.sync.dma_start(x_words[:].bitcast(I32), xt_words[0].rearrange("p c r -> p (c r)").bitcast(I32))
        on_sync = [nc.sync] * 4
        load_scale_rows(on_sync, w_plane, w_scales)
        nc.sync.dma_start(put[:], offs3)
        nc.sync.dma_start(w2_raw[:].bitcast(I32), w2_words[0].rearrange("p c r -> p (c r)").bitcast(I32))
        load_scale_rows([nc.gpsimd] * 2 + [nc.sync] * 2, w2_plane, w2_scales)
        nc.sync.dma_start(read[:], offs4)
        nc.sync.dma_start(ws_sb[:].bitcast(I32), ws_words[0].bitcast(I32))
        nc.sync.dma_start(wb_sb[:].bitcast(I32), wb_words[0].bitcast(I32))
        load_scale_rows(on_sync, ws_plane, ws_scales)
        load_scale_rows(on_sync, wb_plane, wb_scales)

        w_dealt = tile("w_dealt", [2 * R], U8)
        w2_dealt = tile("w2_dealt", [R], U32)
        plane_dealt = tile("plane_dealt", [R], U8)

        def deal(copy, dealt, raw):
            copy(dealt.rearrange("p (t m) -> p t m", t=PACK), raw.rearrange("p (m t) -> p t m", t=PACK))

        def deal_words(dealt, raw):
            nc.scalar.copy(dealt.rearrange("p (t m) -> p m t", t=PACK), raw.rearrange("p (m t) -> p m t", t=PACK))

        x1 = tile("x1", [J], U32)
        s1 = tile("s1", [J], U8)
        s2 = tile("s2", [J], U8)

        deal_words(w_dealt[:].bitcast(U16), w_raw[:].bitcast(U16))
        nc.vector.tensor_copy(s1[:], x_plane[:].indirect(first[:]))
        nc.vector.tensor_copy(s2[:], x_plane[:].indirect(second[:]))
        nc.vector.tensor_copy(x1[:], x_words[:].indirect(first[:]))
        for t0 in range(2):
            nc.vector.tensor_copy(
                plane_dealt[:].rearrange("p (t m) -> p t m", t=PACK)[:, t0::2, :],
                w_plane[:].rearrange("p (m t) -> p t m", t=PACK)[:, t0::2, :])
        x2 = tile("x2", [J], U32, "early")
        nc.vector.tensor_copy(x2[:], x_words[:].indirect(second[:]))
        deal_words(w2_dealt[:], w2_raw[:])

        a_ps = [ps.tile([P, J], F32, name="a_ps%d" % t, tag="a_ps%d" % t) for t in range(PACK)]
        a_even = tile("a_even", [2 * J], F32, "raw")
        plane2_dealt = tile("plane2_dealt", [R], U8)
        deal(nc.vector.tensor_copy, plane2_dealt[:], w2_plane[:])
        a_odd = tile("a_odd", [2 * J], F32, "late")
        a_sb = [(a_even, a_odd)[t % 2][:, J * (t // 2) : J * (t // 2 + 1)] for t in range(PACK)]
        for t in (0, 2, 1, 3):
            nc.tensor.matmul_mx(
                a_ps[t][:], lhsT=w_dealt[:, 2 * P * t : 2 * P * (t + 1)].bitcast(E2M1),
                lhsT_scale=plane_dealt[:, P * t : P * (t + 1)],
                rhs=x1[:].bitcast(E5M2), rhs_scale=s1[:], start=True, stop=True)

        def on_scalar(dst, src):
            nc.scalar.activation(dst, src, COPY)

        on_vector = nc.vector.tensor_copy

        def leave(move, t):
            move(a_sb[t], a_ps[t][:])

        def place(move, t):
            move(boards[t][:].indirect(put[:]), a_sb[t])

        picked = [tile("picked%d" % h, [PACK, HALF], F32) for h in range(2)]

        def pick(move, t, h):
            cols = LIST_COLS // 2
            move(picked[h][:, t, :], boards[t][:].indirect(read[:, cols * h : cols * (h + 1)]))

        for step in (leave, place):
            for t in range(PACK):
                step((on_scalar, on_vector)[t % 2], t)

        b_ps = [ps.tile([P, PACK, HALF], F32, name="b_ps%d" % h) for h in range(2)]
        y_tags = [["y_ps0", "y_ps1"], ["a_ps0", "a_ps1"]]
        y_ps = [[ps.tile([P, HALF], F32, name="y_ps%d%d" % (h, n), tag=y_tags[h][n]) for n in range(2)] for h in range(2)]
        halves = [slice(HALF * h, HALF * (h + 1)) for h in range(2)]
        for h in range(2):
            for t in range(PACK):
                nc.tensor.matmul_mx(
                    b_ps[h][:, t, :], lhsT=w2_dealt[:, P * t : P * (t + 1)].bitcast(E4M3),
                    lhsT_scale=plane2_dealt[:, P * t : P * (t + 1)],
                    rhs=x2[:, halves[h]].bitcast(E5M2), rhs_scale=s2[:, halves[h]], start=True, stop=True)
        for h in range(2):
            for n in range(2):
                nc.tensor.matmul_mx(
                    y_ps[h][n][:], lhsT=ws_sb[:, 2 * P * n : 2 * P * (n + 1)].bitcast(E2M1),
                    lhsT_scale=ws_plane[:, P * n : P * (n + 1)],
                    rhs=x1[:, halves[h]].bitcast(E5M2), rhs_scale=s1[:, halves[h]], start=True, stop=False)

        hid = [tile("hid%d" % h, [PACK * HALF], BF16) for h in range(2)]
        codes = [tile("codes%d" % h, [HALF], U32) for h in range(2)]
        h_plane = [tile("h_plane%d" % h, [HALF], U8) for h in range(2)]
        y_sb = [tile("y_sb%d" % h, [2, HALF], F32) for h in range(2)]
        out_v = out.rearrange("(n p) j -> p n j", p=P)

        def larger(h):
            nc.vector.tensor_tensor(
                hid[h][:].rearrange("p (c i t) -> p c t i", i=4, t=PACK),
                picked[h][:].rearrange("p t (c i) -> p c t i", i=4),
                b_ps[h][:].rearrange("p t (c i) -> p c t i", i=4), MAX)

        def finish(h):
            nc.vector.quantize_mx(codes[h][:].bitcast(E4M3), h_plane[h][:], hid[h][:])
            for n in range(2):
                nc.tensor.matmul_mx(
                    y_ps[h][n][:], lhsT=wb_sb[:, 2 * P * n : 2 * P * (n + 1)].bitcast(E2M1),
                    lhsT_scale=wb_plane[:, P * n : P * (n + 1)],
                    rhs=codes[h][:].bitcast(E4M3), rhs_scale=h_plane[h][:], start=False, stop=True)

        def store(h):
            on_scalar(y_sb[h][:, 0, :], y_ps[h][0][:])
            on_vector(y_sb[h][:, 1, :], y_ps[h][1][:])
            nc.sync.dma_start(out_v[:, :, halves[h]], y_sb[h][:])

        for h in range(2):
            for t in range(PACK):
                pick(on_vector if t == 3 or (t, h) == (1, 0) else on_scalar, t, h)
        for step in (larger, finish, store):
            for h in range(2):
                step(h)
